import numpy as np
import ml_dtypes


def mxq(x, axis, fmt="e4m3"):
    dtype, down = {"e4m3": (ml_dtypes.float8_e4m3fn, 7), "e5m2": (ml_dtypes.float8_e5m2, 14)}[fmt]
    v = np.moveaxis(np.asarray(x, np.float32).astype(ml_dtypes.bfloat16).astype(np.float64), axis, -1)
    blocks = v.reshape(v.shape[:-1] + (-1, 32))
    amax = np.abs(blocks).max(-1, keepdims=True)
    byte = np.maximum(np.where(amax > 0, np.frexp(amax)[1] - 1 + 127, 0) - down, 1)
    scale = np.exp2(byte - 127.0)
    codes = (blocks / scale).astype(np.float32).astype(dtype).astype(np.float64)
    return np.moveaxis((codes * scale).reshape(v.shape), -1, axis)


WIDE = False


def mx_kscale(k):
    if not WIDE:
        return np.ones(k)
    levels = np.array([10, -10, 5, -5, 0])
    if k % 512:
        return np.exp2(np.random.permutation(np.resize(levels, k // 32))).repeat(32)
    a = np.empty((k // 512, 16))
    for p in range(k // 512):
        a[p, :8] = np.random.permutation(np.resize(levels, 8))
        for g in range(8):
            far = levels[np.abs(levels - a[p, g]) >= 10]
            a[p, g + 8] = far[np.random.randint(len(far))]
    return np.exp2(a.ravel()).repeat(32)


def f64(x):
    return np.asarray(x).astype(np.float64)


def striped(idx):
    return np.tile(idx.reshape(-1, 16).T, (8, 1)).astype(np.uint16)


def unstriped(offs):
    return offs[:16].T.reshape(-1).astype(np.int64)


def striped8(idx):
    return np.concatenate([x.reshape(-1, 16).T for x in idx]).astype(np.uint16)


def runs(offs, k):
    lists = np.stack([offs[16 * r : 16 * r + 16].T.reshape(-1) for r in range(8)]).astype(np.int64)
    return lists[np.arange(k) % 512 // 64]


def pack_weight(w):
    k, n = w.shape
    w = f64(np.asarray(w, np.float32).astype(ml_dtypes.bfloat16)).reshape(k // 32, 32, n)
    amax = np.abs(w).max(1)
    byte = np.clip(np.where(amax > 0, np.frexp(amax)[1] - 1 + 127 - 7, 1), 1, 254)
    scaled = (w * np.exp2(127.0 - byte)[:, None, :]).reshape(k, n).astype(np.float32)
    words = np.ascontiguousarray(scaled.reshape(k // 512, 128, 4, n).transpose(0, 1, 3, 2)).astype(ml_dtypes.float8_e4m3fn).view(np.uint8)
    return words, np.ascontiguousarray(byte.astype(np.uint8).reshape(k // 512, 16, n))


def unpack_weight(words, scales):
    g, p, n, _ = words.shape
    vals = np.ascontiguousarray(words).view(ml_dtypes.float8_e4m3fn).astype(np.float64) * np.repeat(np.exp2(scales.astype(np.float64) - 127.0), 8, axis=1)[..., None]
    return vals.transpose(0, 1, 3, 2).reshape(g * 512, n)


def relu(v):
    return np.maximum(v, 0.0)


K, T, S, N, H = 512, 2048, 512, 512, 512
P = 2 ** 7


def setup_inputs():
    n = np.random.standard_normal
    s = mx_kscale(K)[:, None]
    u = mx_kscale(S)
    packed_xT = pack_weight(n((K, T)) * s)
    return {
        "x_words": packed_xT[0],
        "x_scales": packed_xT[1],
        "wa": (n((K, H)) / np.sqrt(K) / s).astype(np.float32),
        "c1": np.tile(np.random.uniform(0.3, 0.9, H), (P, 1)).astype(np.float32),
        "c2": np.tile(np.random.uniform(0.3, 0.9, H), (P, 1)).astype(np.float32),
        "c3": np.tile(np.random.uniform(0.3, 0.9, H), (P, 1)).astype(np.float32),
        "gt": (np.random.uniform(0.5, 1.5, (S, 1)) * u[:, None]).astype(np.float32),
        "w1": (n((S, N)) / np.sqrt(S) / u[:, None]).astype(np.float32),
        "offs": striped(np.random.permutation(T)[:S]),
        "f1": striped8(np.stack([np.random.permutation(H) for _ in range(8)])),
        "f2": striped8(np.stack([np.random.permutation(H) for _ in range(8)])),
        "f3": striped8(np.stack([np.random.permutation(H) for _ in range(8)])),
    }


def reference(x_words, x_scales, wa, c1, c2, c3, gt, w1, offs, f1, f2, f3):
    xq = unpack_weight(x_words, x_scales)[:, unstriped(offs)]
    y = xq.T @ mxq(f64(wa), 0, "e4m3")
    z = f64(gt) * (relu(f64(c1)[:1] * (y[np.arange(S)[:, None], runs(f1, S)]) + f64(c2)[:1] * (y[np.arange(S)[:, None], runs(f2, S)]) + f64(c3)[:1] * (y[np.arange(S)[:, None], runs(f3, S)])))
    return mxq(f64(w1), 0, "e4m3").T @ mxq(z, 0, "e4m3")

@@ -1,0 +1,175 @@
+from contextlib import ExitStack
+
+import concourse.mybir as mybir
+from concourse.masks import make_identity
+
+K, T, S, H, N = 512, 2048, 512, 512, 512
+FLOPS = 2 * K * S * H + 2 * S * N * H
+
+F32 = mybir.dt.float32
+BF16 = mybir.dt.bfloat16
+I32 = mybir.dt.int32
+U32 = mybir.dt.uint32
+U16 = mybir.dt.uint16
+U8 = mybir.dt.uint8
+FP8X4 = mybir.dt.float8_e4m3fn_x4
+ALU = mybir.AluOpType
+ACT = mybir.ActivationFunctionType
+
+P = 128
+PACK = 4
+HALF = H // 2
+VECTOR_SHARE = 160
+CHUNKS = ((0, 256), (256, 384), (384, 512))
+
+
+def interleaved(raw, grouped, lo, hi):
+    src = raw[:, :, lo:hi].rearrange("p t (c i) -> p c t i", i=4)
+    dst = grouped[:, lo:hi, :].rearrange("p (c i) t -> p c t i", i=4)
+    return dst, src
+
+
+def tile_picked_feattap_relu_p_kernel(tc, x_words, x_scales, wa, c1, c2, c3, gt, w1, offs, f1, f2, f3, out):
+    nc = tc.nc
+    with ExitStack() as ctx:
+        keep = ctx.enter_context(tc.tile_pool(name="keep", bufs=1))
+        psum = ctx.enter_context(tc.psum_pool(name="psum", bufs=1))
+
+        x_table = keep.tile([P, T], I32, name="x_table")
+        nc.sync.dma_start(x_table[:], x_words[0].rearrange("p n t -> p (n t)").bitcast(I32))
+        picks = keep.tile([P, S // 16], U16, name="picks")
+        nc.sync.dma_start(picks[:], offs)
+
+        scale_table = keep.tile([P, T], U8, name="scale_table")
+        nc.vector.memset(scale_table[:].bitcast(I32), 0)
+        for q in range(4):
+            nc.scalar.dma_start(
+                scale_table[32 * q : 32 * q + 4, :].bitcast(I32),
+                x_scales[0, 4 * q : 4 * q + 4, :].bitcast(I32),
+            )
+
+        gate = keep.tile([P, PACK], F32, name="gate")
+        nc.gpsimd.dma_start(gate[:], gt.rearrange("(p t) o -> p (t o)", t=PACK))
+
+        wa_rows = wa.rearrange("(p t) h -> p t h", t=PACK)
+        wa_raw = []
+        for h in range(2):
+            raw = keep.tile([P, PACK, HALF], F32, name=f"wa_raw{h}")
+            nc.sync.dma_start(raw[:], wa_rows[:, :, h * HALF : (h + 1) * HALF])
+            wa_raw.append(raw)
+
+        taps, weights = [], []
+        for k, (f, c) in enumerate(((f1, c1), (f2, c2), (f3, c3))):
+            tap = keep.tile([P, H // 16], U16, name=f"tap{k}")
+            nc.sync.dma_start(tap[:], f)
+            weight = keep.tile([P, H], F32, name=f"weight{k}")
+            nc.sync.dma_start(weight[:], c)
+            taps.append(tap)
+            weights.append(weight)
+
+        w1_raw = keep.tile([P, PACK, N], F32, name="w1_raw")
+        nc.sync.dma_start(w1_raw[:], w1.rearrange("(p t) n -> p t n", t=PACK))
+
+        gate_abs = keep.tile([P, PACK], F32, name="gate_abs")
+        nc.scalar.activation(gate_abs[:], gate[:], ACT.Abs)
+        gate_step = keep.tile([P, PACK], F32, name="gate_step")
+        nc.gpsimd.tensor_scalar(gate_step[:], gate[:], 0.0, 2.0, ALU.is_ge, ALU.mult)
+        gate_sign = keep.tile([P, PACK], F32, name="gate_sign")
+        nc.gpsimd.tensor_scalar(gate_sign[:], gate_step[:], 1.0, -1.0, ALU.mult, ALU.add)
+        ident = keep.tile([P, P], F32, name="ident")
+        make_identity(nc, ident[:])
+
+        picked_scales = keep.tile([P, S], U8, name="picked_scales")
+        nc.vector.tensor_copy(picked_scales[:], scale_table[:].indirect(picks[:]))
+        x_scale = keep.tile([P, PACK, P], U8, name="x_scale", align_bytes=64)
+        nc.vector.tensor_copy(x_scale[:].rearrange("p t m -> p m t"), picked_scales[:].rearrange("p (m t) -> p m t", t=PACK))
+        picked_words = keep.tile([P, S], U32, name="picked_words")
+        nc.vector.tensor_copy(picked_words[:], x_table[:].bitcast(U32).indirect(picks[:]))
+        x_codes = keep.tile([P, PACK, P], U32, name="x_codes", align_bytes=64)
+        nc.vector.tensor_copy(x_codes[:].rearrange("p t m -> p m t"), picked_words[:].rearrange("p (m t) -> p m t", t=PACK))
+
+        wa_codes = keep.tile([P, H], U32, name="wa_codes", align_bytes=64)
+        wa_scale = keep.tile([P, H], U8, name="wa_scale", align_bytes=64)
+        for h in range(2):
+            grouped = keep.tile([P, HALF, PACK], BF16, name=f"wa_grouped{h}", align_bytes=64)
+            if h == 0:
+                nc.scalar.copy(*interleaved(wa_raw[h], grouped, 0, HALF))
+            else:
+                nc.vector.tensor_copy(*interleaved(wa_raw[h], grouped, 0, VECTOR_SHARE))
+                nc.scalar.copy(*interleaved(wa_raw[h], grouped, VECTOR_SHARE, HALF))
+            cols = slice(h * HALF, (h + 1) * HALF)
+            nc.vector.quantize_mx(wa_codes[:, cols].bitcast(FP8X4), wa_scale[:, cols], grouped[:].rearrange("p w t -> p (w t)"))
+
+        y = []
+        for t in range(PACK):
+            y_t = keep.tile([P, H], F32, name=f"y{t}")
+            pieces = ((0, HALF), (HALF, H)) if t == 0 else ((0, H),)
+            for lo, hi in pieces:
+                bank = psum.tile([P, hi - lo], F32, tag="y_bank", bufs=2, name="y_bank")
+                nc.tensor.matmul_mx(
+                    bank[:], lhsT=x_codes[:, t, :].bitcast(FP8X4), lhsT_scale=x_scale[:, t, :],
+                    rhs=wa_codes[:, lo:hi].bitcast(FP8X4), rhs_scale=wa_scale[:, lo:hi], start=True, stop=True,
+                )
+                nc.scalar.activation(y_t[:, lo:hi], bank[:], ACT.Copy, scale=gate_abs[:, t : t + 1])
+            y.append(y_t)
+
+        w1_signed = keep.tile([P, PACK, N], BF16, name="w1_signed")
+        w1_grouped = keep.tile([P, N, PACK], BF16, name="w1_grouped", align_bytes=64)
+        w1_codes = keep.tile([P, N], U32, name="w1_codes", align_bytes=64)
+        w1_scale = keep.tile([P, N], U8, name="w1_scale", align_bytes=64)
+
+        def prepare_w1():
+            for t in range(PACK):
+                nc.scalar.activation(w1_signed[:, t, :], w1_raw[:, t, :], ACT.Copy, scale=gate_sign[:, t : t + 1])
+            for lo in range(0, N, P):
+                nc.scalar.copy(*interleaved(w1_signed, w1_grouped, lo, lo + P))
+            nc.vector.quantize_mx(w1_codes[:].bitcast(FP8X4), w1_scale[:], w1_grouped[:].rearrange("p w t -> p (w t)"))
+
+        out_rows = out.rearrange("(a p) j -> p a j", p=P)
+
+        for ci, (lo, hi) in enumerate(CHUNKS):
+            width = hi - lo
+            blocks = width // P
+            sums = [psum.tile([P, PACK, P], F32, tag="sum_bank", bufs=3, name="sum_bank") for b in range(blocks)]
+            turned = psum.tile([P, blocks, 2, P], F32, tag="turned_bank", bufs=1, name="turned_bank")
+            for t in range(PACK):
+                for k in range(3):
+                    tapped = keep.tile([P, width], F32, name=f"tapped{ci}_{t}_{k}")
+                    nc.vector.tensor_tensor(
+                        tapped[:], y[t][:].indirect(taps[k][:, lo // 16 : hi // 16]), weights[k][:, lo:hi], ALU.mult
+                    )
+                    for b in range(blocks):
+                        nc.tensor.matmul(
+                            sums[b][:, t, :], lhsT=tapped[:, b * P : (b + 1) * P], rhs=ident[:],
+                            is_transpose=True, start=(k == 0), stop=(k == 2),
+                        )
+                if t % 2 == 1:
+                    u = t // 2
+                    for b in range(blocks):
+                        pairs = keep.tile([P, P, 2], BF16, name=f"pairs{ci}_{b}_{u}")
+                        nc.scalar.activation(pairs[:], sums[b][:, 2 * u : 2 * u + 2, :].rearrange("j e p -> j p e"), ACT.Relu)
+                        nc.tensor.transpose(turned[:, b, u, :], pairs[:].rearrange("j p e -> j (p e)").bitcast(F32), ident[:])
+                if ci == 0 and t == 0:
+                    prepare_w1()
+
+            z_grouped = keep.tile([P, blocks, P, 2], F32, name=f"z_grouped{ci}", align_bytes=64)
+            nc.scalar.copy(z_grouped[:], turned[:].rearrange("p b u j -> p b j u"))
+            z_codes = keep.tile([P, width], U32, name=f"z_codes{ci}", align_bytes=64)
+            z_scale = keep.tile([P, width], U8, name=f"z_scale{ci}", align_bytes=64)
+            nc.vector.quantize_mx(
+                z_codes[:].bitcast(FP8X4), z_scale[:], z_grouped[:].rearrange("p b j u -> p (b j u)").bitcast(BF16)
+            )
+            result = keep.tile([P, PACK, width], F32, name=f"result{ci}")
+            for a0 in (0, 2):
+                bank = psum.tile([P, 2, width], F32, tag="out_bank", bufs=2, name="out_bank")
+                for a in range(2):
+                    m_cols = slice((a0 + a) * P, (a0 + a + 1) * P)
+                    nc.tensor.matmul_mx(
+                        bank[:, a, :], lhsT=w1_codes[:, m_cols].bitcast(FP8X4), lhsT_scale=w1_scale[:, m_cols],
+                        rhs=z_codes[:].bitcast(FP8X4), rhs_scale=z_scale[:], start=True, stop=True,
+                    )
+                if ci == len(CHUNKS) - 1 and a0 == 0:
+                    nc.vector.tensor_copy(result[:, a0 : a0 + 2, :], bank[:])
+                else:
+                    nc.scalar.copy(result[:, a0 : a0 + 2, :], bank[:])
+            nc.sync.dma_start(out_rows[:, :, lo:hi], result[:])

@@ -19,8 +19,8 @@ ACT = mybir.ActivationFunctionType
 P = 128
 PACK = 4
 HALF = H // 2
-VECTOR_SHARE = 160
 CHUNKS = ((0, 256), (256, 384), (384, 512))
+RUNS = ({0: 4}, {0: 2, 2: 2}, {0: 3, 3: 1})
 
 
 def interleaved(raw, grouped, lo, hi):
@@ -33,20 +33,20 @@ def tile_picked_feattap_relu_p_kernel(tc, x_words, x_scales, wa, c1, c2, c3, gt,
     nc = tc.nc
     with ExitStack() as ctx:
         keep = ctx.enter_context(tc.tile_pool(name="keep", bufs=1))
+        head = ctx.enter_context(tc.tile_pool(name="head", bufs=1))
         psum = ctx.enter_context(tc.psum_pool(name="psum", bufs=1))
 
-        x_table = keep.tile([P, T], I32, name="x_table")
-        nc.sync.dma_start(x_table[:], x_words[0].rearrange("p n t -> p (n t)").bitcast(I32))
-        picks = keep.tile([P, S // 16], U16, name="picks")
-        nc.sync.dma_start(picks[:], offs)
-
         scale_table = keep.tile([P, T], U8, name="scale_table")
-        nc.vector.memset(scale_table[:].bitcast(I32), 0)
+        nc.gpsimd.memset(scale_table[:].bitcast(I32), 0)
         for q in range(4):
             nc.scalar.dma_start(
                 scale_table[32 * q : 32 * q + 4, :].bitcast(I32),
                 x_scales[0, 4 * q : 4 * q + 4, :].bitcast(I32),
             )
+        picks = keep.tile([P, S // 16], U16, name="picks")
+        nc.sync.dma_start(picks[:], offs)
+        x_table = keep.tile([P, T], I32, name="x_table")
+        nc.sync.dma_start(x_table[:], x_words[0].rearrange("p n t -> p (n t)").bitcast(I32))
 
         gate = keep.tile([P, PACK], F32, name="gate")
         nc.gpsimd.dma_start(gate[:], gt.rearrange("(p t) o -> p (t o)", t=PACK))
@@ -67,38 +67,41 @@ def tile_picked_feattap_relu_p_kernel(tc, x_words, x_scales, wa, c1, c2, c3, gt,
             taps.append(tap)
             weights.append(weight)
 
-        w1_raw = keep.tile([P, PACK, N], F32, name="w1_raw")
-        nc.sync.dma_start(w1_raw[:], w1.rearrange("(p t) n -> p t n", t=PACK))
+        w1_rows = w1.rearrange("(p t) n -> p t n", t=PACK)
+        w1_raw = []
+        for t in range(PACK):
+            raw = keep.tile([P, N], F32, name=f"w1_raw{t}")
+            nc.sync.dma_start(raw[:], w1_rows[:, t, :])
+            w1_raw.append(raw)
 
-        gate_abs = keep.tile([P, PACK], F32, name="gate_abs")
-        nc.scalar.activation(gate_abs[:], gate[:], ACT.Abs)
+        ident = keep.tile([P, P], F32, name="ident")
+        make_identity(nc, ident[:])
         gate_step = keep.tile([P, PACK], F32, name="gate_step")
         nc.gpsimd.tensor_scalar(gate_step[:], gate[:], 0.0, 2.0, ALU.is_ge, ALU.mult)
         gate_sign = keep.tile([P, PACK], F32, name="gate_sign")
         nc.gpsimd.tensor_scalar(gate_sign[:], gate_step[:], 1.0, -1.0, ALU.mult, ALU.add)
-        ident = keep.tile([P, P], F32, name="ident")
-        make_identity(nc, ident[:])
+        gate_abs = keep.tile([P, PACK], F32, name="gate_abs", tag="slot_gate")
+        nc.gpsimd.tensor_tensor(gate_abs[:], gate[:], gate_sign[:], ALU.mult)
 
-        picked_scales = keep.tile([P, S], U8, name="picked_scales")
+        picked_scales = head.tile([P, S], U8, name="picked_scales", offset=512)
         nc.vector.tensor_copy(picked_scales[:], scale_table[:].indirect(picks[:]))
         x_scale = keep.tile([P, PACK, P], U8, name="x_scale", align_bytes=64)
         nc.vector.tensor_copy(x_scale[:].rearrange("p t m -> p m t"), picked_scales[:].rearrange("p (m t) -> p m t", t=PACK))
-        picked_words = keep.tile([P, S], U32, name="picked_words")
+        picked_words = head.tile([P, S], U32, name="picked_words", offset=512)
         nc.vector.tensor_copy(picked_words[:], x_table[:].bitcast(U32).indirect(picks[:]))
         x_codes = keep.tile([P, PACK, P], U32, name="x_codes", align_bytes=64)
         nc.vector.tensor_copy(x_codes[:].rearrange("p t m -> p m t"), picked_words[:].rearrange("p (m t) -> p m t", t=PACK))
 
         wa_codes = keep.tile([P, H], U32, name="wa_codes", align_bytes=64)
-        wa_scale = keep.tile([P, H], U8, name="wa_scale", align_bytes=64)
+        wa_scale = head.tile([P, H], U8, name="wa_scale", align_bytes=64, offset=1024)
         for h in range(2):
-            grouped = keep.tile([P, HALF, PACK], BF16, name=f"wa_grouped{h}", align_bytes=64)
-            if h == 0:
-                nc.scalar.copy(*interleaved(wa_raw[h], grouped, 0, HALF))
-            else:
-                nc.vector.tensor_copy(*interleaved(wa_raw[h], grouped, 0, VECTOR_SHARE))
-                nc.scalar.copy(*interleaved(wa_raw[h], grouped, VECTOR_SHARE, HALF))
-            cols = slice(h * HALF, (h + 1) * HALF)
-            nc.vector.quantize_mx(wa_codes[:, cols].bitcast(FP8X4), wa_scale[:, cols], grouped[:].rearrange("p w t -> p (w t)"))
+            by_vector = head.tile([P, P, PACK], BF16, name=f"wa_by_vector{h}", align_bytes=64, offset=1536 * h)
+            by_scalar = keep.tile([P, P, PACK], BF16, name=f"wa_by_scalar{h}", align_bytes=64)
+            nc.vector.tensor_copy(*interleaved(wa_raw[h][:, :, :P], by_vector, 0, P))
+            nc.scalar.copy(*interleaved(wa_raw[h][:, :, P:], by_scalar, 0, P))
+            for q, grouped in enumerate((by_vector, by_scalar)):
+                cols = slice(h * HALF + q * P, h * HALF + (q + 1) * P)
+                nc.vector.quantize_mx(wa_codes[:, cols].bitcast(FP8X4), wa_scale[:, cols], grouped[:].rearrange("p w t -> p (w t)"))
 
         y = []
         for t in range(PACK):
@@ -110,56 +113,60 @@ def tile_picked_feattap_relu_p_kernel(tc, x_words, x_scales, wa, c1, c2, c3, gt,
                     bank[:], lhsT=x_codes[:, t, :].bitcast(FP8X4), lhsT_scale=x_scale[:, t, :],
                     rhs=wa_codes[:, lo:hi].bitcast(FP8X4), rhs_scale=wa_scale[:, lo:hi], start=True, stop=True,
                 )
-                nc.scalar.activation(y_t[:, lo:hi], bank[:], ACT.Copy, scale=gate_abs[:, t : t + 1])
+                if lo > 0:
+                    nc.vector.tensor_scalar(y_t[:, lo:hi], bank[:], gate_abs[:, t : t + 1], None, ALU.mult)
+                else:
+                    nc.scalar.activation(y_t[:, lo:hi], bank[:], ACT.Copy, scale=gate_abs[:, t : t + 1])
             y.append(y_t)
 
-        w1_signed = keep.tile([P, PACK, N], BF16, name="w1_signed")
-        w1_grouped = keep.tile([P, N, PACK], BF16, name="w1_grouped", align_bytes=64)
+        w1_signed = keep.tile([P, PACK, N], BF16, name="w1_signed", tag="slot_gate")
+        w1_grouped = keep.tile([P, N, PACK], BF16, name="w1_grouped", tag="slot_1_2", align_bytes=64)
         w1_codes = keep.tile([P, N], U32, name="w1_codes", align_bytes=64)
         w1_scale = keep.tile([P, N], U8, name="w1_scale", align_bytes=64)
 
-        def prepare_w1():
-            for t in range(PACK):
-                nc.scalar.activation(w1_signed[:, t, :], w1_raw[:, t, :], ACT.Copy, scale=gate_sign[:, t : t + 1])
-            for lo in range(0, N, P):
-                nc.scalar.copy(*interleaved(w1_signed, w1_grouped, lo, lo + P))
-            nc.vector.quantize_mx(w1_codes[:].bitcast(FP8X4), w1_scale[:], w1_grouped[:].rearrange("p w t -> p (w t)"))
+        for t in range(PACK):
+            nc.scalar.activation(w1_signed[:, t, :], w1_raw[t][:], ACT.Copy, scale=gate_sign[:, t : t + 1])
+        for lo in range(0, N, P):
+            nc.scalar.copy(*interleaved(w1_signed, w1_grouped, lo, lo + P))
+        nc.vector.quantize_mx(w1_codes[:].bitcast(FP8X4), w1_scale[:], w1_grouped[:].rearrange("p w t -> p (w t)"))
 
         out_rows = out.rearrange("(a p) j -> p a j", p=P)
 
         for ci, (lo, hi) in enumerate(CHUNKS):
             width = hi - lo
             blocks = width // P
-            sums = [psum.tile([P, PACK, P], F32, tag="sum_bank", bufs=3, name="sum_bank") for b in range(blocks)]
             turned = psum.tile([P, blocks, 2, P], F32, tag="turned_bank", bufs=1, name="turned_bank")
-            for t in range(PACK):
-                for k in range(3):
-                    tapped = keep.tile([P, width], F32, name=f"tapped{ci}_{t}_{k}")
-                    nc.vector.tensor_tensor(
-                        tapped[:], y[t][:].indirect(taps[k][:, lo // 16 : hi // 16]), weights[k][:, lo:hi], ALU.mult
-                    )
-                    for b in range(blocks):
-                        nc.tensor.matmul(
-                            sums[b][:, t, :], lhsT=tapped[:, b * P : (b + 1) * P], rhs=ident[:],
-                            is_transpose=True, start=(k == 0), stop=(k == 2),
+            tapped = []
+            for u in range(2):
+                sums = psum.tile([P, blocks, 2, P], F32, tag="sum_bank", bufs=3, name="sum_bank")
+                for e in range(2):
+                    t = 2 * u + e
+                    if t in RUNS[ci]:
+                        run = keep.tile([P, RUNS[ci][t], 3, width], F32, name=f"tapped{ci}_{t}", tag=f"slot_{ci}_{t}", align_bytes=64)
+                        tapped.extend(run[:, i] for i in range(RUNS[ci][t]))
+                    for k in range(3):
+                        nc.vector.tensor_tensor(
+                            tapped[t][:, k, :], y[t][:].indirect(taps[k][:, lo // 16 : hi // 16]), weights[k][:, lo:hi], ALU.mult
                         )
-                if t % 2 == 1:
-                    u = t // 2
                     for b in range(blocks):
-                        pairs = keep.tile([P, P, 2], BF16, name=f"pairs{ci}_{b}_{u}")
-                        nc.scalar.activation(pairs[:], sums[b][:, 2 * u : 2 * u + 2, :].rearrange("j e p -> j p e"), ACT.Relu)
-                        nc.tensor.transpose(turned[:, b, u, :], pairs[:].rearrange("j p e -> j (p e)").bitcast(F32), ident[:])
-                if ci == 0 and t == 0:
-                    prepare_w1()
+                        for k in range(3):
+                            nc.tensor.matmul(
+                                sums[:, b, e, :], lhsT=tapped[t][:, k, b * P : (b + 1) * P], rhs=ident[:],
+                                is_transpose=True, start=(k == 0), stop=(k == 2),
+                            )
+                pairs = keep.tile([P, blocks, P, 2], BF16, name=f"pairs{ci}_{u}")
+                nc.scalar.activation(pairs[:], sums[:].rearrange("j b e p -> j b p e"), ACT.Relu)
+                for b in range(blocks):
+                    nc.tensor.transpose(turned[:, b, u, :], pairs[:, b].rearrange("j p e -> j (p e)").bitcast(F32), ident[:])
 
-            z_grouped = keep.tile([P, blocks, P, 2], F32, name=f"z_grouped{ci}", align_bytes=64)
+            z_grouped = keep.tile([P, blocks, P, 2], F32, name=f"z_grouped{ci}", tag=("slot_2_0", "slot_2_3", "slot_z")[ci], align_bytes=64)
             nc.scalar.copy(z_grouped[:], turned[:].rearrange("p b u j -> p b j u"))
             z_codes = keep.tile([P, width], U32, name=f"z_codes{ci}", align_bytes=64)
             z_scale = keep.tile([P, width], U8, name=f"z_scale{ci}", align_bytes=64)
             nc.vector.quantize_mx(
                 z_codes[:].bitcast(FP8X4), z_scale[:], z_grouped[:].rearrange("p b j u -> p (b j u)").bitcast(BF16)
             )
-            result = keep.tile([P, PACK, width], F32, name=f"result{ci}")
+            last = ci == len(CHUNKS) - 1
             for a0 in (0, 2):
                 bank = psum.tile([P, 2, width], F32, tag="out_bank", bufs=2, name="out_bank")
                 for a in range(2):
@@ -168,8 +175,9 @@ def tile_picked_feattap_relu_p_kernel(tc, x_words, x_scales, wa, c1, c2, c3, gt,
                         bank[:, a, :], lhsT=w1_codes[:, m_cols].bitcast(FP8X4), lhsT_scale=w1_scale[:, m_cols],
                         rhs=z_codes[:].bitcast(FP8X4), rhs_scale=z_scale[:], start=True, stop=True,
                     )
-                if ci == len(CHUNKS) - 1 and a0 == 0:
-                    nc.vector.tensor_copy(result[:, a0 : a0 + 2, :], bank[:])
+                result = keep.tile([P, 2, width], F32, name=f"result{ci}_{a0}")
+                if last and a0 == 0:
+                    nc.vector.tensor_copy(result[:], bank[:])
                 else:
-                    nc.scalar.copy(result[:, a0 : a0 + 2, :], bank[:])
-            nc.sync.dma_start(out_rows[:, :, lo:hi], result[:])
+                    nc.scalar.copy(result[:], bank[:])
+                nc.sync.dma_start(out_rows[:, a0 : a0 + 2, lo:hi], result[:])

@@ -24,39 +24,36 @@ RUNS = ({0: 4}, {0: 2, 2: 2}, {0: 3, 3: 1})
 
 
 def interleaved(raw, grouped, lo, hi):
-    src = raw[:, :, lo:hi].rearrange("p t (c i) -> p c t i", i=4)
-    dst = grouped[:, lo:hi, :].rearrange("p (c i) t -> p c t i", i=4)
-    return dst, src
+    return grouped, raw[:, :, lo:hi].rearrange("p t w -> p w t")
 
 
 def tile_picked_feattap_relu_p_kernel(tc, x_words, x_scales, wa, c1, c2, c3, gt, w1, offs, f1, f2, f3, out):
     nc = tc.nc
     with ExitStack() as ctx:
         keep = ctx.enter_context(tc.tile_pool(name="keep", bufs=1))
-        head = ctx.enter_context(tc.tile_pool(name="head", bufs=1))
         psum = ctx.enter_context(tc.psum_pool(name="psum", bufs=1))
 
+        wa_rows = wa.rearrange("(p t) h -> p t h", t=PACK)
+        wa_early = keep.tile([P, PACK, HALF], F32, name="wa_early")
+        nc.sync.dma_start(wa_early[:], wa_rows[:, :, :HALF])
+
         scale_table = keep.tile([P, T], U8, name="scale_table")
-        nc.gpsimd.memset(scale_table[:].bitcast(I32), 0)
+        nc.gpsimd.memset(scale_table[:, : T // 2].bitcast(I32), 0)
+        nc.vector.memset(scale_table[:, T // 2 :].bitcast(I32), 0)
         for q in range(4):
-            nc.scalar.dma_start(
+            nc.sync.dma_start(
                 scale_table[32 * q : 32 * q + 4, :].bitcast(I32),
                 x_scales[0, 4 * q : 4 * q + 4, :].bitcast(I32),
             )
         picks = keep.tile([P, S // 16], U16, name="picks")
         nc.sync.dma_start(picks[:], offs)
+        gate = keep.tile([P, PACK], F32, name="gate")
+        nc.sync.dma_start(gate[:], gt.rearrange("(p t) o -> p (t o)", t=PACK))
+
         x_table = keep.tile([P, T], I32, name="x_table")
         nc.sync.dma_start(x_table[:], x_words[0].rearrange("p n t -> p (n t)").bitcast(I32))
-
-        gate = keep.tile([P, PACK], F32, name="gate")
-        nc.gpsimd.dma_start(gate[:], gt.rearrange("(p t) o -> p (t o)", t=PACK))
-
-        wa_rows = wa.rearrange("(p t) h -> p t h", t=PACK)
-        wa_raw = []
-        for h in range(2):
-            raw = keep.tile([P, PACK, HALF], F32, name=f"wa_raw{h}")
-            nc.sync.dma_start(raw[:], wa_rows[:, :, h * HALF : (h + 1) * HALF])
-            wa_raw.append(raw)
+        wa_late = keep.tile([P, PACK, HALF], F32, name="wa_late")
+        nc.sync.dma_start(wa_late[:], wa_rows[:, :, HALF:])
 
         taps, weights = [], []
         for k, (f, c) in enumerate(((f1, c1), (f2, c2), (f3, c3))):
@@ -76,32 +73,31 @@ def tile_picked_feattap_relu_p_kernel(tc, x_words, x_scales, wa, c1, c2, c3, gt,
 
         ident = keep.tile([P, P], F32, name="ident")
         make_identity(nc, ident[:])
-        gate_step = keep.tile([P, PACK], F32, name="gate_step")
-        nc.gpsimd.tensor_scalar(gate_step[:], gate[:], 0.0, 2.0, ALU.is_ge, ALU.mult)
-        gate_sign = keep.tile([P, PACK], F32, name="gate_sign")
-        nc.gpsimd.tensor_scalar(gate_sign[:], gate_step[:], 1.0, -1.0, ALU.mult, ALU.add)
         gate_abs = keep.tile([P, PACK], F32, name="gate_abs", tag="slot_gate")
-        nc.gpsimd.tensor_tensor(gate_abs[:], gate[:], gate_sign[:], ALU.mult)
-
-        picked_scales = head.tile([P, S], U8, name="picked_scales", offset=512)
-        nc.vector.tensor_copy(picked_scales[:], scale_table[:].indirect(picks[:]))
-        x_scale = keep.tile([P, PACK, P], U8, name="x_scale", align_bytes=64)
-        nc.vector.tensor_copy(x_scale[:].rearrange("p t m -> p m t"), picked_scales[:].rearrange("p (m t) -> p m t", t=PACK))
-        picked_words = head.tile([P, S], U32, name="picked_words", offset=512)
-        nc.vector.tensor_copy(picked_words[:], x_table[:].bitcast(U32).indirect(picks[:]))
-        x_codes = keep.tile([P, PACK, P], U32, name="x_codes", align_bytes=64)
-        nc.vector.tensor_copy(x_codes[:].rearrange("p t m -> p m t"), picked_words[:].rearrange("p (m t) -> p m t", t=PACK))
+        nc.scalar.activation(gate_abs[:], gate[:], ACT.Abs)
 
         wa_codes = keep.tile([P, H], U32, name="wa_codes", align_bytes=64)
-        wa_scale = head.tile([P, H], U8, name="wa_scale", align_bytes=64, offset=1024)
-        for h in range(2):
-            by_vector = head.tile([P, P, PACK], BF16, name=f"wa_by_vector{h}", align_bytes=64, offset=1536 * h)
-            by_scalar = keep.tile([P, P, PACK], BF16, name=f"wa_by_scalar{h}", align_bytes=64)
-            nc.vector.tensor_copy(*interleaved(wa_raw[h][:, :, :P], by_vector, 0, P))
-            nc.scalar.copy(*interleaved(wa_raw[h][:, :, P:], by_scalar, 0, P))
-            for q, grouped in enumerate((by_vector, by_scalar)):
-                cols = slice(h * HALF + q * P, h * HALF + (q + 1) * P)
-                nc.vector.quantize_mx(wa_codes[:, cols].bitcast(FP8X4), wa_scale[:, cols], grouped[:].rearrange("p w t -> p (w t)"))
+        wa_scale = keep.tile([P, H], U8, name="wa_scale", align_bytes=64)
+
+        def quantize_wa(copy, raw, first, lo, hi):
+            grouped = keep.tile([P, hi - lo, PACK], BF16, name=f"wa_grouped{lo}", align_bytes=64)
+            copy(*interleaved(raw, grouped[:], lo - first, hi - first))
+            nc.vector.quantize_mx(wa_codes[:, lo:hi].bitcast(FP8X4), wa_scale[:, lo:hi], grouped[:].rearrange("p w t -> p (w t)"))
+
+        quantize_wa(nc.scalar.copy, wa_early, 0, 0, HALF)
+
+        picked_scales = keep.tile([P, S], U8, name="picked_scales")
+        nc.vector.tensor_copy(picked_scales[:], scale_table[:].indirect(picks[:]))
+        x_scale = keep.tile([P, PACK, P], U8, name="x_scale", align_bytes=64)
+        nc.vector.tensor_copy(x_scale[:], picked_scales[:].rearrange("p (m t) -> p t m", t=PACK))
+        picked_words = keep.tile([P, S], U32, name="picked_words")
+        nc.vector.tensor_copy(picked_words[:], x_table[:].bitcast(U32).indirect(picks[:]))
+        x_codes = keep.tile([P, PACK, P], U32, name="x_codes", align_bytes=64)
+        nc.vector.tensor_copy(
+            x_codes[:].rearrange("p t (b i) -> p b t i", i=4), picked_words[:].rearrange("p (b i t) -> p b t i", i=4, t=PACK)
+        )
+        quantize_wa(nc.vector.tensor_copy, wa_late, HALF, HALF, HALF + P)
+        quantize_wa(nc.scalar.copy, wa_late, HALF, HALF + P, H)
 
         y = []
         for t in range(PACK):
@@ -119,6 +115,10 @@ def tile_picked_feattap_relu_p_kernel(tc, x_words, x_scales, wa, c1, c2, c3, gt,
                     nc.scalar.activation(y_t[:, lo:hi], bank[:], ACT.Copy, scale=gate_abs[:, t : t + 1])
             y.append(y_t)
 
+        gate_unit = keep.tile([P, PACK], F32, name="gate_unit", tag="slot_gate")
+        nc.scalar.activation(gate_unit[:], gate[:], ACT.Sign)
+        gate_sign = keep.tile([P, PACK], F32, name="gate_sign")
+        nc.scalar.activation(gate_sign[:], gate_unit[:], ACT.Sign, scale=2.0, bias=1.0)
         w1_signed = keep.tile([P, PACK, N], BF16, name="w1_signed", tag="slot_gate")
         w1_grouped = keep.tile([P, N, PACK], BF16, name="w1_grouped", tag="slot_1_2", align_bytes=64)
         w1_codes = keep.tile([P, N], U32, name="w1_codes", align_bytes=64)
@@ -127,11 +127,34 @@ def tile_picked_feattap_relu_p_kernel(tc, x_words, x_scales, wa, c1, c2, c3, gt,
         for t in range(PACK):
             nc.scalar.activation(w1_signed[:, t, :], w1_raw[t][:], ACT.Copy, scale=gate_sign[:, t : t + 1])
         for lo in range(0, N, P):
-            nc.scalar.copy(*interleaved(w1_signed, w1_grouped, lo, lo + P))
-        nc.vector.quantize_mx(w1_codes[:].bitcast(FP8X4), w1_scale[:], w1_grouped[:].rearrange("p w t -> p (w t)"))
+            nc.scalar.copy(*interleaved(w1_signed, w1_grouped[:, lo : lo + P, :], lo, lo + P))
 
         out_rows = out.rearrange("(a p) j -> p a j", p=P)
 
+        def second_product(ci, z_grouped):
+            lo, hi = CHUNKS[ci]
+            width = hi - lo
+            z_codes = keep.tile([P, width], U32, name=f"z_codes{ci}", align_bytes=64)
+            z_scale = keep.tile([P, width], U8, name=f"z_scale{ci}", align_bytes=64)
+            nc.vector.quantize_mx(
+                z_codes[:].bitcast(FP8X4), z_scale[:], z_grouped[:].rearrange("p b j u -> p (b j u)").bitcast(BF16)
+            )
+            for a0 in (0, 2):
+                bank = psum.tile([P, 2, width], F32, tag="out_bank", bufs=2, name="out_bank")
+                for a in range(2):
+                    m_cols = slice((a0 + a) * P, (a0 + a + 1) * P)
+                    nc.tensor.matmul_mx(
+                        bank[:, a, :], lhsT=w1_codes[:, m_cols].bitcast(FP8X4), lhsT_scale=w1_scale[:, m_cols],
+                        rhs=z_codes[:].bitcast(FP8X4), rhs_scale=z_scale[:], start=True, stop=True,
+                    )
+                result = keep.tile([P, 2, width], F32, name=f"result{ci}_{a0}")
+                if ci == len(CHUNKS) - 1 and a0 == 0:
+                    nc.vector.tensor_copy(result[:], bank[:])
+                else:
+                    nc.scalar.copy(result[:], bank[:])
+                nc.sync.dma_start(out_rows[:, a0 : a0 + 2, lo:hi], result[:])
+
+        z_tiles = []
         for ci, (lo, hi) in enumerate(CHUNKS):
             width = hi - lo
             blocks = width // P
@@ -141,6 +164,12 @@ def tile_picked_feattap_relu_p_kernel(tc, x_words, x_scales, wa, c1, c2, c3, gt,
                 sums = psum.tile([P, blocks, 2, P], F32, tag="sum_bank", bufs=3, name="sum_bank")
                 for e in range(2):
                     t = 2 * u + e
+                    if (ci, t) == (1, 2):
+                        nc.vector.quantize_mx(w1_codes[:].bitcast(FP8X4), w1_scale[:], w1_grouped[:].rearrange("p w t -> p (w t)"))
+                    if (ci, t) == (2, 0):
+                        second_product(0, z_tiles[0])
+                    if (ci, t) == (2, 3):
+                        second_product(1, z_tiles[1])
                     if t in RUNS[ci]:
                         run = keep.tile([P, RUNS[ci][t], 3, width], F32, name=f"tapped{ci}_{t}", tag=f"slot_{ci}_{t}", align_bytes=64)
                         tapped.extend(run[:, i] for i in range(RUNS[ci][t]))
@@ -159,25 +188,7 @@ def tile_picked_feattap_relu_p_kernel(tc, x_words, x_scales, wa, c1, c2, c3, gt,
                 for b in range(blocks):
                     nc.tensor.transpose(turned[:, b, u, :], pairs[:, b].rearrange("j p e -> j (p e)").bitcast(F32), ident[:])
 
-            z_grouped = keep.tile([P, blocks, P, 2], F32, name=f"z_grouped{ci}", tag=("slot_2_0", "slot_2_3", "slot_z")[ci], align_bytes=64)
+            z_grouped = keep.tile([P, blocks, P, 2], F32, name=f"z_grouped{ci}", tag=("slot_2_0", "slot_2_3", "slot_z2")[ci], align_bytes=64)
             nc.scalar.copy(z_grouped[:], turned[:].rearrange("p b u j -> p b j u"))
-            z_codes = keep.tile([P, width], U32, name=f"z_codes{ci}", align_bytes=64)
-            z_scale = keep.tile([P, width], U8, name=f"z_scale{ci}", align_bytes=64)
-            nc.vector.quantize_mx(
-                z_codes[:].bitcast(FP8X4), z_scale[:], z_grouped[:].rearrange("p b j u -> p (b j u)").bitcast(BF16)
-            )
-            last = ci == len(CHUNKS) - 1
-            for a0 in (0, 2):
-                bank = psum.tile([P, 2, width], F32, tag="out_bank", bufs=2, name="out_bank")
-                for a in range(2):
-                    m_cols = slice((a0 + a) * P, (a0 + a + 1) * P)
-                    nc.tensor.matmul_mx(
-                        bank[:, a, :], lhsT=w1_codes[:, m_cols].bitcast(FP8X4), lhsT_scale=w1_scale[:, m_cols],
-                        rhs=z_codes[:].bitcast(FP8X4), rhs_scale=z_scale[:], start=True, stop=True,
-                    )
-                result = keep.tile([P, 2, width], F32, name=f"result{ci}_{a0}")
-                if last and a0 == 0:
-                    nc.vector.tensor_copy(result[:], bank[:])
-                else:
-                    nc.scalar.copy(result[:], bank[:])
-                nc.sync.dma_start(out_rows[:, a0 : a0 + 2, lo:hi], result[:])
+            z_tiles.append(z_grouped)
+        second_product(2, z_tiles[2])

@@ -20,7 +20,7 @@ P = 128
 PACK = 4
 HALF = H // 2
 CHUNKS = ((0, 256), (256, 384), (384, 512))
-RUNS = ({0: 4}, {0: 2, 2: 2}, {0: 3, 3: 1})
+RUNS = ({0: 4}, {0: 4}, {0: 1, 1: 1, 2: 2})
 
 
 def interleaved(raw, grouped, lo, hi):
@@ -75,6 +75,10 @@ def tile_picked_feattap_relu_p_kernel(tc, x_words, x_scales, wa, c1, c2, c3, gt,
         make_identity(nc, ident[:])
         gate_abs = keep.tile([P, PACK], F32, name="gate_abs", tag="slot_gate")
         nc.scalar.activation(gate_abs[:], gate[:], ACT.Abs)
+        gate_unit = keep.tile([P, PACK], F32, name="gate_unit")
+        nc.scalar.activation(gate_unit[:], gate[:], ACT.Sign)
+        gate_sign = keep.tile([P, PACK], F32, name="gate_sign")
+        nc.scalar.activation(gate_sign[:], gate_unit[:], ACT.Sign, scale=2.0, bias=1.0)
 
         wa_codes = keep.tile([P, H], U32, name="wa_codes", align_bytes=64)
         wa_scale = keep.tile([P, H], U8, name="wa_scale", align_bytes=64)
@@ -96,7 +100,7 @@ def tile_picked_feattap_relu_p_kernel(tc, x_words, x_scales, wa, c1, c2, c3, gt,
         nc.vector.tensor_copy(
             x_codes[:].rearrange("p t (b i) -> p b t i", i=4), picked_words[:].rearrange("p (b i t) -> p b t i", i=4, t=PACK)
         )
-        quantize_wa(nc.vector.tensor_copy, wa_late, HALF, HALF, HALF + P)
+        quantize_wa(nc.scalar.copy, wa_late, HALF, HALF, HALF + P)
         quantize_wa(nc.scalar.copy, wa_late, HALF, HALF + P, H)
 
         y = []
@@ -104,7 +108,7 @@ def tile_picked_feattap_relu_p_kernel(tc, x_words, x_scales, wa, c1, c2, c3, gt,
             y_t = keep.tile([P, H], F32, name=f"y{t}")
             pieces = ((0, HALF), (HALF, H)) if t == 0 else ((0, H),)
             for lo, hi in pieces:
-                bank = psum.tile([P, hi - lo], F32, tag="y_bank", bufs=2, name="y_bank")
+                bank = psum.tile([P, hi - lo], F32, tag="product_bank", bufs=2, name="y_bank")
                 nc.tensor.matmul_mx(
                     bank[:], lhsT=x_codes[:, t, :].bitcast(FP8X4), lhsT_scale=x_scale[:, t, :],
                     rhs=wa_codes[:, lo:hi].bitcast(FP8X4), rhs_scale=wa_scale[:, lo:hi], start=True, stop=True,
@@ -115,19 +119,15 @@ def tile_picked_feattap_relu_p_kernel(tc, x_words, x_scales, wa, c1, c2, c3, gt,
                     nc.scalar.activation(y_t[:, lo:hi], bank[:], ACT.Copy, scale=gate_abs[:, t : t + 1])
             y.append(y_t)
 
-        gate_unit = keep.tile([P, PACK], F32, name="gate_unit", tag="slot_gate")
-        nc.scalar.activation(gate_unit[:], gate[:], ACT.Sign)
-        gate_sign = keep.tile([P, PACK], F32, name="gate_sign")
-        nc.scalar.activation(gate_sign[:], gate_unit[:], ACT.Sign, scale=2.0, bias=1.0)
         w1_signed = keep.tile([P, PACK, N], BF16, name="w1_signed", tag="slot_gate")
-        w1_grouped = keep.tile([P, N, PACK], BF16, name="w1_grouped", tag="slot_1_2", align_bytes=64)
+        w1_grouped = keep.tile([P, N, PACK], BF16, name="w1_grouped", tag="slot_2_0", align_bytes=64)
         w1_codes = keep.tile([P, N], U32, name="w1_codes", align_bytes=64)
         w1_scale = keep.tile([P, N], U8, name="w1_scale", align_bytes=64)
 
         for t in range(PACK):
             nc.scalar.activation(w1_signed[:, t, :], w1_raw[t][:], ACT.Copy, scale=gate_sign[:, t : t + 1])
-        for lo in range(0, N, P):
-            nc.scalar.copy(*interleaved(w1_signed, w1_grouped[:, lo : lo + P, :], lo, lo + P))
+        for lo in range(0, N, HALF):
+            nc.scalar.copy(*interleaved(w1_signed, w1_grouped[:, lo : lo + HALF, :], lo, lo + HALF))
 
         out_rows = out.rearrange("(a p) j -> p a j", p=P)
 
@@ -139,36 +139,38 @@ def tile_picked_feattap_relu_p_kernel(tc, x_words, x_scales, wa, c1, c2, c3, gt,
             nc.vector.quantize_mx(
                 z_codes[:].bitcast(FP8X4), z_scale[:], z_grouped[:].rearrange("p b j u -> p (b j u)").bitcast(BF16)
             )
-            for a0 in (0, 2):
-                bank = psum.tile([P, 2, width], F32, tag="out_bank", bufs=2, name="out_bank")
-                for a in range(2):
+            group = PACK if ci == 1 else 2
+            for a0 in range(0, PACK, group):
+                bank = psum.tile([P, group, width], F32, tag="product_bank", bufs=2, name="out_bank")
+                for a in range(group):
                     m_cols = slice((a0 + a) * P, (a0 + a + 1) * P)
                     nc.tensor.matmul_mx(
                         bank[:, a, :], lhsT=w1_codes[:, m_cols].bitcast(FP8X4), lhsT_scale=w1_scale[:, m_cols],
                         rhs=z_codes[:].bitcast(FP8X4), rhs_scale=z_scale[:], start=True, stop=True,
                     )
-                result = keep.tile([P, 2, width], F32, name=f"result{ci}_{a0}")
+                result = keep.tile([P, group, width], F32, name=f"result{ci}_{a0}")
                 if ci == len(CHUNKS) - 1 and a0 == 0:
                     nc.vector.tensor_copy(result[:], bank[:])
                 else:
                     nc.scalar.copy(result[:], bank[:])
-                nc.sync.dma_start(out_rows[:, a0 : a0 + 2, lo:hi], result[:])
+                queue = nc.scalar if ci == len(CHUNKS) - 1 and a0 == 2 else nc.sync
+                queue.dma_start(out_rows[:, a0 : a0 + group, lo:hi], result[:])
 
         z_tiles = []
         for ci, (lo, hi) in enumerate(CHUNKS):
             width = hi - lo
             blocks = width // P
-            turned = psum.tile([P, blocks, 2, P], F32, tag="turned_bank", bufs=1, name="turned_bank")
+            turned = psum.tile([P, blocks, 2, P], F32, tag="turned_bank", bufs=2, name="turned_bank")
             tapped = []
             for u in range(2):
-                sums = psum.tile([P, blocks, 2, P], F32, tag="sum_bank", bufs=3, name="sum_bank")
+                sums = psum.tile([P, blocks, 2, P], F32, tag="sum_bank", bufs=4, name="sum_bank")
                 for e in range(2):
                     t = 2 * u + e
-                    if (ci, t) == (1, 2):
-                        nc.vector.quantize_mx(w1_codes[:].bitcast(FP8X4), w1_scale[:], w1_grouped[:].rearrange("p w t -> p (w t)"))
                     if (ci, t) == (2, 0):
+                        nc.vector.quantize_mx(w1_codes[:].bitcast(FP8X4), w1_scale[:], w1_grouped[:].rearrange("p w t -> p (w t)"))
+                    if (ci, t) == (2, 1):
                         second_product(0, z_tiles[0])
-                    if (ci, t) == (2, 3):
+                    if (ci, t) == (2, 2):
                         second_product(1, z_tiles[1])
                     if t in RUNS[ci]:
                         run = keep.tile([P, RUNS[ci][t], 3, width], F32, name=f"tapped{ci}_{t}", tag=f"slot_{ci}_{t}", align_bytes=64)
@@ -188,7 +190,7 @@ def tile_picked_feattap_relu_p_kernel(tc, x_words, x_scales, wa, c1, c2, c3, gt,
                 for b in range(blocks):
                     nc.tensor.transpose(turned[:, b, u, :], pairs[:, b].rearrange("j p e -> j (p e)").bitcast(F32), ident[:])
 
-            z_grouped = keep.tile([P, blocks, P, 2], F32, name=f"z_grouped{ci}", tag=("slot_2_0", "slot_2_3", "slot_z2")[ci], align_bytes=64)
+            z_grouped = keep.tile([P, blocks, P, 2], F32, name=f"z_grouped{ci}", tag=("slot_2_1", "slot_2_2", "slot_z2")[ci], align_bytes=64)
             nc.scalar.copy(z_grouped[:], turned[:].rearrange("p b u j -> p b j u"))
             z_tiles.append(z_grouped)
         second_product(2, z_tiles[2])

from contextlib import ExitStack

import concourse.mybir as mybir
from concourse.masks import make_identity

K, T, S, H, N = 512, 2048, 512, 512, 512
FLOPS = 2 * K * S * H + 2 * S * N * H

F32 = mybir.dt.float32
BF16 = mybir.dt.bfloat16
I32 = mybir.dt.int32
U32 = mybir.dt.uint32
U16 = mybir.dt.uint16
U8 = mybir.dt.uint8
FP8X4 = mybir.dt.float8_e4m3fn_x4
ALU = mybir.AluOpType
ACT = mybir.ActivationFunctionType

P = 128
PACK = 4
HALF = H // 2
CHUNKS = ((0, 256), (256, 384), (384, 512))
RUNS = ({0: 4}, {0: 4}, {0: 1, 1: 1, 2: 2})


def interleaved(raw, grouped, lo, hi):
    return grouped, raw[:, :, lo:hi].rearrange("p t w -> p w t")


def tile_picked_feattap_relu_p_kernel(tc, x_words, x_scales, wa, c1, c2, c3, gt, w1, offs, f1, f2, f3, out):
    nc = tc.nc
    with ExitStack() as ctx:
        keep = ctx.enter_context(tc.tile_pool(name="keep", bufs=1))
        psum = ctx.enter_context(tc.psum_pool(name="psum", bufs=1))

        wa_rows = wa.rearrange("(p t) h -> p t h", t=PACK)
        wa_early = keep.tile([P, PACK, HALF], F32, name="wa_early")
        nc.sync.dma_start(wa_early[:], wa_rows[:, :, :HALF])

        scale_table = keep.tile([P, T], U8, name="scale_table")
        nc.gpsimd.memset(scale_table[:, : T // 2].bitcast(I32), 0)
        nc.vector.memset(scale_table[:, T // 2 :].bitcast(I32), 0)
        for q in range(4):
            nc.sync.dma_start(
                scale_table[32 * q : 32 * q + 4, :].bitcast(I32),
                x_scales[0, 4 * q : 4 * q + 4, :].bitcast(I32),
            )
        picks = keep.tile([P, S // 16], U16, name="picks")
        nc.sync.dma_start(picks[:], offs)
        gate = keep.tile([P, PACK], F32, name="gate")
        nc.sync.dma_start(gate[:], gt.rearrange("(p t) o -> p (t o)", t=PACK))

        x_table = keep.tile([P, T], I32, name="x_table")
        nc.sync.dma_start(x_table[:], x_words[0].rearrange("p n t -> p (n t)").bitcast(I32))
        wa_late = keep.tile([P, PACK, HALF], F32, name="wa_late")
        nc.sync.dma_start(wa_late[:], wa_rows[:, :, HALF:])

        taps, weights = [], []
        for k, (f, c) in enumerate(((f1, c1), (f2, c2), (f3, c3))):
            tap = keep.tile([P, H // 16], U16, name=f"tap{k}")
            nc.sync.dma_start(tap[:], f)
            weight = keep.tile([P, H], F32, name=f"weight{k}")
            nc.sync.dma_start(weight[:], c)
            taps.append(tap)
            weights.append(weight)

        w1_rows = w1.rearrange("(p t) n -> p t n", t=PACK)
        w1_raw = []
        for t in range(PACK):
            raw = keep.tile([P, N], F32, name=f"w1_raw{t}")
            nc.sync.dma_start(raw[:], w1_rows[:, t, :])
            w1_raw.append(raw)

        ident = keep.tile([P, P], F32, name="ident")
        make_identity(nc, ident[:])
        gate_abs = keep.tile([P, PACK], F32, name="gate_abs", tag="slot_gate")
        nc.scalar.activation(gate_abs[:], gate[:], ACT.Abs)
        gate_unit = keep.tile([P, PACK], F32, name="gate_unit")
        nc.scalar.activation(gate_unit[:], gate[:], ACT.Sign)
        gate_sign = keep.tile([P, PACK], F32, name="gate_sign")
        nc.scalar.activation(gate_sign[:], gate_unit[:], ACT.Sign, scale=2.0, bias=1.0)

        wa_codes = keep.tile([P, H], U32, name="wa_codes", align_bytes=64)
        wa_scale = keep.tile([P, H], U8, name="wa_scale", align_bytes=64)

        def quantize_wa(copy, raw, first, lo, hi):
            grouped = keep.tile([P, hi - lo, PACK], BF16, name=f"wa_grouped{lo}", align_bytes=64)
            copy(*interleaved(raw, grouped[:], lo - first, hi - first))
            nc.vector.quantize_mx(wa_codes[:, lo:hi].bitcast(FP8X4), wa_scale[:, lo:hi], grouped[:].rearrange("p w t -> p (w t)"))

        quantize_wa(nc.scalar.copy, wa_early, 0, 0, HALF)

        picked_scales = keep.tile([P, S], U8, name="picked_scales")
        nc.vector.tensor_copy(picked_scales[:], scale_table[:].indirect(picks[:]))
        x_scale = keep.tile([P, PACK, P], U8, name="x_scale", align_bytes=64)
        nc.vector.tensor_copy(x_scale[:], picked_scales[:].rearrange("p (m t) -> p t m", t=PACK))
        picked_words = keep.tile([P, S], U32, name="picked_words")
        nc.vector.tensor_copy(picked_words[:], x_table[:].bitcast(U32).indirect(picks[:]))
        x_codes = keep.tile([P, PACK, P], U32, name="x_codes", align_bytes=64)
        nc.vector.tensor_copy(
            x_codes[:].rearrange("p t (b i) -> p b t i", i=4), picked_words[:].rearrange("p (b i t) -> p b t i", i=4, t=PACK)
        )
        quantize_wa(nc.scalar.copy, wa_late, HALF, HALF, HALF + P)
        quantize_wa(nc.scalar.copy, wa_late, HALF, HALF + P, H)

        y = []
        for t in range(PACK):
            y_t = keep.tile([P, H], F32, name=f"y{t}")
            pieces = ((0, HALF), (HALF, H)) if t == 0 else ((0, H),)
            for lo, hi in pieces:
                bank = psum.tile([P, hi - lo], F32, tag="product_bank", bufs=2, name="y_bank")
                nc.tensor.matmul_mx(
                    bank[:], lhsT=x_codes[:, t, :].bitcast(FP8X4), lhsT_scale=x_scale[:, t, :],
                    rhs=wa_codes[:, lo:hi].bitcast(FP8X4), rhs_scale=wa_scale[:, lo:hi], start=True, stop=True,
                )
                if lo > 0:
                    nc.vector.tensor_scalar(y_t[:, lo:hi], bank[:], gate_abs[:, t : t + 1], None, ALU.mult)
                else:
                    nc.scalar.activation(y_t[:, lo:hi], bank[:], ACT.Copy, scale=gate_abs[:, t : t + 1])
            y.append(y_t)

        w1_signed = keep.tile([P, PACK, N], BF16, name="w1_signed", tag="slot_gate")
        w1_grouped = keep.tile([P, N, PACK], BF16, name="w1_grouped", tag="slot_2_0", align_bytes=64)
        w1_codes = keep.tile([P, N], U32, name="w1_codes", align_bytes=64)
        w1_scale = keep.tile([P, N], U8, name="w1_scale", align_bytes=64)

        for t in range(PACK):
            nc.scalar.activation(w1_signed[:, t, :], w1_raw[t][:], ACT.Copy, scale=gate_sign[:, t : t + 1])
        for lo in range(0, N, HALF):
            nc.scalar.copy(*interleaved(w1_signed, w1_grouped[:, lo : lo + HALF, :], lo, lo + HALF))

        out_rows = out.rearrange("(a p) j -> p a j", p=P)

        def second_product(ci, z_grouped):
            lo, hi = CHUNKS[ci]
            width = hi - lo
            z_codes = keep.tile([P, width], U32, name=f"z_codes{ci}", align_bytes=64)
            z_scale = keep.tile([P, width], U8, name=f"z_scale{ci}", align_bytes=64)
            nc.vector.quantize_mx(
                z_codes[:].bitcast(FP8X4), z_scale[:], z_grouped[:].rearrange("p b j u -> p (b j u)").bitcast(BF16)
            )
            group = PACK if ci == 1 else 2
            for a0 in range(0, PACK, group):
                bank = psum.tile([P, group, width], F32, tag="product_bank", bufs=2, name="out_bank")
                for a in range(group):
                    m_cols = slice((a0 + a) * P, (a0 + a + 1) * P)
                    nc.tensor.matmul_mx(
                        bank[:, a, :], lhsT=w1_codes[:, m_cols].bitcast(FP8X4), lhsT_scale=w1_scale[:, m_cols],
                        rhs=z_codes[:].bitcast(FP8X4), rhs_scale=z_scale[:], start=True, stop=True,
                    )
                result = keep.tile([P, group, width], F32, name=f"result{ci}_{a0}")
                if ci == len(CHUNKS) - 1 and a0 == 0:
                    nc.vector.tensor_copy(result[:], bank[:])
                else:
                    nc.scalar.copy(result[:], bank[:])
                queue = nc.scalar if ci == len(CHUNKS) - 1 and a0 == 2 else nc.sync
                queue.dma_start(out_rows[:, a0 : a0 + group, lo:hi], result[:])

        z_tiles = []
        for ci, (lo, hi) in enumerate(CHUNKS):
            width = hi - lo
            blocks = width // P
            turned = psum.tile([P, blocks, 2, P], F32, tag="turned_bank", bufs=2, name="turned_bank")
            tapped = []
            for u in range(2):
                sums = psum.tile([P, blocks, 2, P], F32, tag="sum_bank", bufs=4, name="sum_bank")
                for e in range(2):
                    t = 2 * u + e
                    if (ci, t) == (2, 0):
                        nc.vector.quantize_mx(w1_codes[:].bitcast(FP8X4), w1_scale[:], w1_grouped[:].rearrange("p w t -> p (w t)"))
                    if (ci, t) == (2, 1):
                        second_product(0, z_tiles[0])
                    if (ci, t) == (2, 2):
                        second_product(1, z_tiles[1])
                    if t in RUNS[ci]:
                        run = keep.tile([P, RUNS[ci][t], 3, width], F32, name=f"tapped{ci}_{t}", tag=f"slot_{ci}_{t}", align_bytes=64)
                        tapped.extend(run[:, i] for i in range(RUNS[ci][t]))
                    for k in range(3):
                        nc.vector.tensor_tensor(
                            tapped[t][:, k, :], y[t][:].indirect(taps[k][:, lo // 16 : hi // 16]), weights[k][:, lo:hi], ALU.mult
                        )
                    for b in range(blocks):
                        for k in range(3):
                            nc.tensor.matmul(
                                sums[:, b, e, :], lhsT=tapped[t][:, k, b * P : (b + 1) * P], rhs=ident[:],
                                is_transpose=True, start=(k == 0), stop=(k == 2),
                            )
                pairs = keep.tile([P, blocks, P, 2], BF16, name=f"pairs{ci}_{u}")
                nc.scalar.activation(pairs[:], sums[:].rearrange("j b e p -> j b p e"), ACT.Relu)
                for b in range(blocks):
                    nc.tensor.transpose(turned[:, b, u, :], pairs[:, b].rearrange("j p e -> j (p e)").bitcast(F32), ident[:])

            z_grouped = keep.tile([P, blocks, P, 2], F32, name=f"z_grouped{ci}", tag=("slot_2_1", "slot_2_2", "slot_z2")[ci], align_bytes=64)
            nc.scalar.copy(z_grouped[:], turned[:].rearrange("p b u j -> p b j u"))
            z_tiles.append(z_grouped)
        second_product(2, z_tiles[2])
